import numpy as np
import ml_dtypes


def mxq(x, axis, fmt="e4m3"):
    dtype, down = {"e4m3": (ml_dtypes.float8_e4m3fn, 7), "e5m2": (ml_dtypes.float8_e5m2, 14)}[fmt]
    v = np.moveaxis(np.asarray(x, np.float32).astype(ml_dtypes.bfloat16).astype(np.float64), axis, -1)
    blocks = v.reshape(v.shape[:-1] + (-1, 32))
    amax = np.abs(blocks).max(-1, keepdims=True)
    byte = np.maximum(np.where(amax > 0, np.frexp(amax)[1] - 1 + 127, 0) - down, 1)
    scale = np.exp2(byte - 127.0)
    codes = (blocks / scale).astype(np.float32).astype(dtype).astype(np.float64)
    return np.moveaxis((codes * scale).reshape(v.shape), -1, axis)


WIDE = False


def mx_kscale(k):
    if not WIDE:
        return np.ones(k)
    levels = np.array([10, -10, 5, -5, 0])
    if k % 512:
        return np.exp2(np.random.permutation(np.resize(levels, k // 32))).repeat(32)
    a = np.empty((k // 512, 16))
    for p in range(k // 512):
        a[p, :8] = np.random.permutation(np.resize(levels, 8))
        for g in range(8):
            far = levels[np.abs(levels - a[p, g]) >= 10]
            a[p, g + 8] = far[np.random.randint(len(far))]
    return np.exp2(a.ravel()).repeat(32)


def f64(x):
    return np.asarray(x).astype(np.float64)


def striped(idx):
    return np.tile(np.asarray(idx).reshape(-1, 16).T, (8, 1)).astype(np.uint16)


def unstriped(offs):
    return offs[:16].T.reshape(-1).astype(np.int64)


E2M1 = np.array([0.0, 0.5, 1.0, 1.5, 2.0, 3.0, 4.0, 6.0, -0.0, -0.5, -1.0, -1.5, -2.0, -3.0, -4.0, -6.0])


def pack_weight(w, fmt):
    k, n = w.shape
    w = f64(np.asarray(w, np.float32).astype(ml_dtypes.bfloat16)).reshape(k // 32, 32, n)
    amax = np.abs(w).max(1)
    if fmt == "e4m3":
        byte = np.frexp(amax)[1] - 1 + 127 - 7
    else:
        mant, ex = np.frexp(amax / 6.0)
        byte = np.where(mant > 0.5, ex, ex - 1) + 127
    byte = np.clip(np.where(amax > 0, byte, 1), 1, 254)
    scaled = (w * np.exp2(127.0 - byte)[:, None, :]).reshape(k, n).astype(np.float32)
    by_word = np.ascontiguousarray(scaled.reshape(k // 512, 128, 4, n).transpose(0, 1, 3, 2))
    if fmt == "e4m3":
        words = by_word.astype(ml_dtypes.float8_e4m3fn).view(np.uint8)
    else:
        c = by_word.astype(ml_dtypes.float4_e2m1fn).view(np.uint8) & 0xF
        words = (c[..., 0::2] | (c[..., 1::2] << 4)).reshape(k // 512, 128, 2 * n)
    return np.ascontiguousarray(words), np.ascontiguousarray(byte.astype(np.uint8).reshape(k // 512, 16, n))


def unpack_weight(words, scales, fmt):
    g, _, n = scales.shape
    words = np.ascontiguousarray(words).reshape(g, 128, n, -1)
    if fmt == "e4m3":
        vals = words.view(ml_dtypes.float8_e4m3fn).astype(np.float64)
    else:
        nib = np.empty((g, 128, n, 4), np.uint8)
        nib[..., 0::2] = words & 0xF
        nib[..., 1::2] = words >> 4
        vals = E2M1[nib]
    vals = vals * np.repeat(np.exp2(scales.astype(np.float64) - 127.0), 8, axis=1)[..., None]
    return vals.transpose(0, 1, 3, 2).reshape(g * 512, n)


D, E, T, I, Q = 512, 512, 2048, 512, 128


def setup_inputs():
    n = np.random.standard_normal
    idx = np.random.permutation(T)[:I]
    fd = mx_kscale(D)
    fi = mx_kscale(I)
    ti = np.ones(T)
    ti[idx] = fi
    keysp = pack_weight(n((D, T)) / fd[:, None], "e4m3")
    return {
        "query": (n((D, Q)) * 0.35 / np.sqrt(D) * fd[:, None]).astype(np.float32),
        "dquery": (n((D, Q)) * 0.6 / np.sqrt(D) * fd[:, None]).astype(np.float32),
        "query2": (n((D, Q)) * 0.35 / np.sqrt(D) * fd[:, None]).astype(np.float32),
        "dquery2": (n((D, Q)) * 0.6 / np.sqrt(D) * fd[:, None]).astype(np.float32),
        "keys_words": keysp[0],
        "keys_scales": keysp[1],
        "os": (np.random.uniform(4.0, 16.0, (1, I)) * fi).astype(np.float32),
        "vals": (n((E, T)) / ti).astype(np.float32),
        "offs": striped(idx),
    }


def reference(query, dquery, query2, dquery2, keys_words, keys_scales, os, vals, offs):
    idx = unstriped(offs)
    keysu = unpack_weight(keys_words, keys_scales, "e4m3")
    queryq = mxq(f64(query), 0, "e4m3")
    keysidxg = keysu[:, idx]
    a = queryq.T @ keysidxg
    dqueryq = mxq(f64(dquery), 0, "e4m3")
    ta = dqueryq.T @ keysidxg
    query2q = mxq(f64(query2), 0, "e4m3")
    b = query2q.T @ keysidxg
    dquery2q = mxq(f64(dquery2), 0, "e4m3")
    tb = dquery2q.T @ keysidxg
    s = a * (b + 1.0)
    p = np.exp(s - np.max(s, axis=1, keepdims=True))
    ts = ta * (b + 1.0) + tb * a
    tp = ts * p
    tw = (tp - np.sum(tp, axis=1, keepdims=True) * p / np.sum(p, axis=1, keepdims=True)) / np.sum(p, axis=1, keepdims=True)
    wo1 = tw * f64(os)
    wt1 = wo1.T
    vt1 = f64(vals)[:, idx].T
    wt1q = mxq(wt1, 0, "e4m3")
    vt1q = mxq(vt1, 0, "e4m3")
    o = wt1q.T @ vt1q
    return o

@@ -1,0 +1,159 @@
+from contextlib import ExitStack
+
+import concourse.mybir as mybir
+from concourse.masks import make_identity
+
+D, E, T, I, Q = 512, 512, 2048, 512, 128
+P = 128
+PACK = 4
+FLOPS = 2 * (4 * D * Q * I + I * Q * E)
+
+F32 = mybir.dt.float32
+BF16 = mybir.dt.bfloat16
+I32 = mybir.dt.int32
+U32 = mybir.dt.uint32
+U16 = mybir.dt.uint16
+U8 = mybir.dt.uint8
+FP8X4 = mybir.dt.float8_e4m3fn_x4
+ALU = mybir.AluOpType
+ACT = mybir.ActivationFunctionType
+AXIS = mybir.AxisListType
+
+
+def tile_attend_ttproductscore_kernel(tc, query, dquery, query2, dquery2, keys_words, keys_scales, factors, vals, offs, out):
+    nc = tc.nc
+    with ExitStack() as ctx:
+        sb = ctx.enter_context(tc.tile_pool(name="sb", bufs=1))
+        ps = ctx.enter_context(tc.psum_pool(name="ps", bufs=1))
+
+        offsets = sb.tile([P, I // 16], U16, name="offsets")
+        nc.sync.dma_start(offsets[:], offs)
+
+        key_bytes = sb.tile([P, T], U8, name="key_bytes", align_bytes=64)
+        nc.gpsimd.memset(key_bytes[:].bitcast(I32), 0)
+
+        def load_query(n, rows):
+            tile = sb.tile([P, PACK, Q], F32, name="q_raw%d" % n)
+            nc.sync.dma_start(tile[:], rows.rearrange("(p j) q -> p j q", j=PACK))
+            return tile
+
+        raw = [load_query(0, query)]
+        for r in range(PACK):
+            nc.sync.dma_start(key_bytes[r:P:32, :].bitcast(I32), keys_scales[0, r:16:PACK, :].bitcast(I32))
+        key_words = sb.tile([P, T], U32, name="key_words", align_bytes=64)
+        nc.sync.dma_start(key_words[:].bitcast(I32), keys_words[0].rearrange("p n t -> p (n t)").bitcast(I32))
+        raw.extend([load_query(1, query2), load_query(2, dquery), load_query(3, dquery2)])
+
+        pools = []
+        for j in range(E // P):
+            tile = sb.tile([P, T], F32, name="vals%d" % j, align_bytes=64)
+            nc.sync.dma_start(tile[:], vals[j * P : (j + 1) * P, :])
+            pools.append(tile)
+            if j == 1:
+                slot_factor = sb.tile([P, PACK], F32, name="slot_factor")
+                nc.sync.dma_start(slot_factor[:], factors.rearrange("o (p t) -> (o p) t", t=PACK))
+
+        identity = sb.tile([P, P], F32, name="identity")
+        make_identity(nc, identity[:])
+
+        def quantize(name, grouped, width, tag=None):
+            codes = sb.tile([P, width], U32, name=name + "_codes", tag=tag or name + "_codes", align_bytes=64)
+            scales = sb.tile([P, width], U8, name=name + "_scales", align_bytes=64)
+            nc.vector.quantize_mx(out=codes[:].bitcast(FP8X4), scales=scales[:], in_=grouped)
+            return codes[:], scales[:]
+
+        def product(bank, stationary, moving):
+            nc.tensor.matmul_mx(
+                out=bank,
+                lhsT=stationary[0].bitcast(FP8X4),
+                lhsT_scale=stationary[1],
+                rhs=moving[0].bitcast(FP8X4),
+                rhs_scale=moving[1],
+                start=True,
+                stop=True,
+            )
+
+        listed_bytes = sb.tile([P, I], U8, name="listed_bytes", align_bytes=64)
+        nc.vector.tensor_copy(listed_bytes[:], key_bytes[:].indirect(offsets[:]))
+        listed_words = sb.tile([P, I], U32, name="listed_words", align_bytes=64)
+        nc.vector.tensor_copy(listed_words[:], key_words[:].indirect(offsets[:]))
+        listed_keys = (listed_words[:], listed_bytes[:])
+
+        scores = []
+        for n in range(4):
+            grouped = sb.tile([P, Q, PACK], BF16, name="q_grouped%d" % n, align_bytes=64)
+            source = raw[n][:].rearrange("p j q -> p q j")
+            if n < 3:
+                nc.scalar.activation(grouped[:], source, ACT.Copy)
+            else:
+                nc.vector.tensor_copy(grouped[:], source)
+            operand = quantize("q%d" % n, grouped[:].rearrange("p q j -> p (q j)"), Q)
+            bank = ps.tile([P, I], F32, name="score%d" % n)
+            product(bank[:], operand, listed_keys)
+            if n % 2 == 0:
+                held = sb.tile([P, I], F32, name="score_sb%d" % n, align_bytes=64)
+                nc.scalar.copy(held[:], bank[:])
+                scores.append(held)
+            else:
+                scores.append(bank)
+        a, b, ta, tb = scores
+
+        s = sb.tile([P, I], F32, name="s")
+        nc.vector.scalar_tensor_tensor(s[:], b[:], 1.0, a[:], ALU.add, ALU.mult)
+        ts_second = sb.tile([P, I], F32, name="ts_second")
+        nc.vector.tensor_tensor(ts_second[:], tb[:], a[:], ALU.mult)
+        neg_max = sb.tile([P, 1], F32, name="neg_max")
+        nc.vector.tensor_reduce(neg_max[:], s[:], AXIS.X, ALU.max, negate=True)
+        p = sb.tile([P, I], F32, name="p")
+        p_sum = sb.tile([P, 1], F32, name="p_sum")
+        nc.scalar.activation(p[:], s[:], ACT.Exp, bias=neg_max[:], accum_out=p_sum[:])
+        ts_first = sb.tile([P, I], F32, name="ts_first", align_bytes=64)
+        nc.vector.scalar_tensor_tensor(ts_first[:], b[:], 1.0, ta[:], ALU.add, ALU.mult)
+        ts = sb.tile([P, I], F32, name="ts", align_bytes=64)
+        nc.vector.tensor_tensor(ts[:], ts_first[:], ts_second[:], ALU.add)
+        inv_sum = sb.tile([P, 1], F32, name="inv_sum")
+        nc.vector.reciprocal(inv_sum[:], p_sum[:])
+        pn = sb.tile([P, I], F32, name="pn")
+        nc.scalar.activation(pn[:], p[:], ACT.Copy, scale=inv_sum[:])
+        tpn = sb.tile([P, I], F32, name="tpn")
+        mean_ts = sb.tile([P, 1], F32, name="mean_ts")
+        nc.vector.scalar_tensor_tensor(tpn[:], ts[:], inv_sum[:], p[:], ALU.mult, ALU.mult, accum_out=mean_ts[:])
+        tw = sb.tile([P, I], F32, name="tw")
+        nc.vector.scalar_tensor_tensor(tw[:], ts[:], mean_ts[:], pn[:], ALU.subtract, ALU.mult)
+
+        tw_turned = ps.tile([P, PACK, Q], F32, name="tw_turned")
+        for t in range(PACK):
+            nc.tensor.transpose(tw_turned[:, t, :], tw[:, t:I:PACK], identity[:])
+        early = sb.tile([P, PACK * I], BF16, name="early", align_bytes=64)
+        w_grouped = early[:, 0:I].rearrange("p (q t) -> p q t", t=PACK)
+        for t in range(PACK):
+            nc.scalar.activation(w_grouped[:, :, t], tw_turned[:, t, :], ACT.Copy, scale=slot_factor[:, t : t + 1])
+
+        def turn_values(j, grouped):
+            listed = sb.tile([P, I], BF16, name="v_listed%d" % j, tag=("score_sb2", "ts", "vals1", "vals2")[j], align_bytes=64)
+            nc.vector.tensor_copy(listed[:], pools[j][:].indirect(offsets[:]))
+            pairs = listed[:].bitcast(F32)
+            turned = ps.tile([P, 2, P], F32, name="v_turned%d" % (j % 2))
+            for u in range(2):
+                nc.tensor.transpose(turned[:, u, :], pairs[:, u : I // 2 : 2], identity[:])
+            nc.scalar.copy(grouped.bitcast(F32).rearrange("p (e u) -> p e u", u=2), turned[:].rearrange("p u e -> p e u"))
+
+        for j in range(3):
+            turn_values(j, early[:, (j + 1) * I : (j + 2) * I])
+        late = sb.tile([P, I], BF16, name="late", align_bytes=64)
+        turn_values(3, late[:])
+        early_codes, early_scales = quantize("early", early[:], I, tag="vals3")
+        late_codes, late_scales = quantize("late", late[:], P)
+
+        weights = (early_codes[:, 0:Q], early_scales[:, 0:Q])
+        pieces = (
+            (0, 2 * P, early_codes[:, Q : Q + 2 * P], early_scales[:, Q : Q + 2 * P]),
+            (2 * P, P, early_codes[:, Q + 2 * P : I], early_scales[:, Q + 2 * P : I]),
+            (3 * P, P, late_codes, late_scales),
+        )
+        for n, (first, width, codes, scales) in enumerate(pieces):
+            bank = ps.tile([P, width], F32, name="score%d" % n)
+            product(bank[:], weights, (codes, scales))
+            result = sb.tile([P, width], F32, name="result%d" % n)
+            nc.scalar.copy(result[:], bank[:])
+            nc.sync.dma_start(out[:, first : first + width], result[:])

@@ -42,14 +42,14 @@ def tile_attend_ttproductscore_kernel(tc, query, dquery, query2, dquery2, keys_w
             nc.sync.dma_start(key_bytes[r:P:32, :].bitcast(I32), keys_scales[0, r:16:PACK, :].bitcast(I32))
         key_words = sb.tile([P, T], U32, name="key_words", align_bytes=64)
         nc.sync.dma_start(key_words[:].bitcast(I32), keys_words[0].rearrange("p n t -> p (n t)").bitcast(I32))
-        raw.extend([load_query(1, query2), load_query(2, dquery), load_query(3, dquery2)])
+        raw.extend([load_query(1, query2), load_query(2, dquery2), load_query(3, dquery)])
 
         pools = []
         for j in range(E // P):
             tile = sb.tile([P, T], F32, name="vals%d" % j, align_bytes=64)
             nc.sync.dma_start(tile[:], vals[j * P : (j + 1) * P, :])
             pools.append(tile)
-            if j == 1:
+            if j == 0:
                 slot_factor = sb.tile([P, PACK], F32, name="slot_factor")
                 nc.sync.dma_start(slot_factor[:], factors.rearrange("o (p t) -> (o p) t", t=PACK))
 
@@ -90,58 +90,74 @@ def tile_attend_ttproductscore_kernel(tc, query, dquery, query2, dquery2, keys_w
             operand = quantize("q%d" % n, grouped[:].rearrange("p q j -> p (q j)"), Q)
             bank = ps.tile([P, I], F32, name="score%d" % n)
             product(bank[:], operand, listed_keys)
-            if n % 2 == 0:
+            if n in (0, 3):
                 held = sb.tile([P, I], F32, name="score_sb%d" % n, align_bytes=64)
                 nc.scalar.copy(held[:], bank[:])
                 scores.append(held)
             else:
                 scores.append(bank)
-        a, b, ta, tb = scores
+        a, b, tb, ta = scores
 
-        s = sb.tile([P, I], F32, name="s")
+        factor_rows = ps.tile([P, PACK, P], F32, name="factor_rows")
+        for t in range(PACK):
+            nc.tensor.transpose(factor_rows[:, t, :], slot_factor[:, t : t + 1].to_broadcast([P, P]), identity[:])
+
+        early = sb.tile([P, PACK * I], BF16, name="early", align_bytes=64)
+        late = sb.tile([P, I], BF16, name="late", align_bytes=64)
+
+        def turn(rows, bank_name, grouped):
+            pairs = rows.bitcast(F32)
+            turned = ps.tile([P, 2, P], F32, name=bank_name)
+            for u in range(2):
+                nc.tensor.transpose(turned[:, u, :], pairs[:, u : I // 2 : 2], identity[:])
+            nc.scalar.copy(grouped.bitcast(F32).rearrange("p (e u) -> p e u", u=2), turned[:].rearrange("p u e -> p e u"))
+
+        def gather_values(j, grouped):
+            listed = sb.tile([P, I], BF16, name="v_listed%d" % j, align_bytes=64)
+            nc.vector.tensor_copy(listed[:], pools[j][:].indirect(offsets[:]))
+            turn(listed[:], "v_turned%d" % (j % 2), grouped)
+
+
+        s = sb.tile([P, I], F32, name="s", align_bytes=64)
         nc.vector.scalar_tensor_tensor(s[:], b[:], 1.0, a[:], ALU.add, ALU.mult)
         ts_second = sb.tile([P, I], F32, name="ts_second")
         nc.vector.tensor_tensor(ts_second[:], tb[:], a[:], ALU.mult)
         neg_max = sb.tile([P, 1], F32, name="neg_max")
         nc.vector.tensor_reduce(neg_max[:], s[:], AXIS.X, ALU.max, negate=True)
-        p = sb.tile([P, I], F32, name="p")
+        p = sb.tile([P, I], F32, name="p", align_bytes=64)
         p_sum = sb.tile([P, 1], F32, name="p_sum")
         nc.scalar.activation(p[:], s[:], ACT.Exp, bias=neg_max[:], accum_out=p_sum[:])
-        ts_first = sb.tile([P, I], F32, name="ts_first", align_bytes=64)
+        ts_first = sb.tile([P, I], F32, name="ts_first")
         nc.vector.scalar_tensor_tensor(ts_first[:], b[:], 1.0, ta[:], ALU.add, ALU.mult)
-        ts = sb.tile([P, I], F32, name="ts", align_bytes=64)
+
+        pool_bf16 = sb.tile([P, T], BF16, name="pool_bf16", tag="s", align_bytes=64)
+        nc.scalar.activation(pool_bf16[:], pools[1][:], ACT.Copy)
+        listed_first = sb.tile([P, I], BF16, name="v_listed1", align_bytes=64)
+        nc.scalar.activation(listed_first[:], pool_bf16[:].indirect(offsets[:]), ACT.Copy)
+        turn(listed_first[:], "v_turned1", early[:, 2 * I : 3 * I])
+
+        gather_values(0, early[:, I : 2 * I])
+        ts = sb.tile([P, I], F32, name="ts")
         nc.vector.tensor_tensor(ts[:], ts_first[:], ts_second[:], ALU.add)
         inv_sum = sb.tile([P, 1], F32, name="inv_sum")
         nc.vector.reciprocal(inv_sum[:], p_sum[:])
-        pn = sb.tile([P, I], F32, name="pn")
-        nc.scalar.activation(pn[:], p[:], ACT.Copy, scale=inv_sum[:])
         tpn = sb.tile([P, I], F32, name="tpn")
         mean_ts = sb.tile([P, 1], F32, name="mean_ts")
         nc.vector.scalar_tensor_tensor(tpn[:], ts[:], inv_sum[:], p[:], ALU.mult, ALU.mult, accum_out=mean_ts[:])
-        tw = sb.tile([P, I], F32, name="tw")
-        nc.vector.scalar_tensor_tensor(tw[:], ts[:], mean_ts[:], pn[:], ALU.subtract, ALU.mult)
-
-        tw_turned = ps.tile([P, PACK, Q], F32, name="tw_turned")
-        for t in range(PACK):
-            nc.tensor.transpose(tw_turned[:, t, :], tw[:, t:I:PACK], identity[:])
-        early = sb.tile([P, PACK * I], BF16, name="early", align_bytes=64)
-        w_grouped = early[:, 0:I].rearrange("p (q t) -> p q t", t=PACK)
-        for t in range(PACK):
-            nc.scalar.activation(w_grouped[:, :, t], tw_turned[:, t, :], ACT.Copy, scale=slot_factor[:, t : t + 1])
-
-        def turn_values(j, grouped):
-            listed = sb.tile([P, I], BF16, name="v_listed%d" % j, tag=("score_sb2", "ts", "vals1", "vals2")[j], align_bytes=64)
-            nc.vector.tensor_copy(listed[:], pools[j][:].indirect(offsets[:]))
-            pairs = listed[:].bitcast(F32)
-            turned = ps.tile([P, 2, P], F32, name="v_turned%d" % (j % 2))
-            for u in range(2):
-                nc.tensor.transpose(turned[:, u, :], pairs[:, u : I // 2 : 2], identity[:])
-            nc.scalar.copy(grouped.bitcast(F32).rearrange("p (e u) -> p e u", u=2), turned[:].rearrange("p u e -> p e u"))
-
-        for j in range(3):
-            turn_values(j, early[:, (j + 1) * I : (j + 2) * I])
-        late = sb.tile([P, I], BF16, name="late", align_bytes=64)
-        turn_values(3, late[:])
+        pno = sb.tile([P, I], F32, name="pno")
+        nc.vector.scalar_tensor_tensor(
+            pno[:].rearrange("p (n t) -> p n t", t=PACK),
+            p[:].rearrange("p (n t) -> p n t", t=PACK),
+            inv_sum[:],
+            factor_rows[:].rearrange("p t n -> p n t"),
+            ALU.mult,
+            ALU.mult,
+        )
+        wo = sb.tile([P, I], BF16, name="wo", align_bytes=64)
+        nc.vector.scalar_tensor_tensor(wo[:], ts[:], mean_ts[:], pno[:], ALU.subtract, ALU.mult)
+        turn(wo[:], "w_turned", early[:, 0:I])
+        gather_values(2, early[:, 3 * I : 4 * I])
+        gather_values(3, late[:])
         early_codes, early_scales = quantize("early", early[:], I, tag="vals3")
         late_codes, late_scales = quantize("late", late[:], P)
 

@@ -26,9 +26,6 @@ def tile_attend_ttproductscore_kernel(tc, query, dquery, query2, dquery2, keys_w
         sb = ctx.enter_context(tc.tile_pool(name="sb", bufs=1))
         ps = ctx.enter_context(tc.psum_pool(name="ps", bufs=1))
 
-        offsets = sb.tile([P, I // 16], U16, name="offsets")
-        nc.sync.dma_start(offsets[:], offs)
-
         key_bytes = sb.tile([P, T], U8, name="key_bytes", align_bytes=64)
         nc.gpsimd.memset(key_bytes[:].bitcast(I32), 0)
 
@@ -38,11 +35,13 @@ def tile_attend_ttproductscore_kernel(tc, query, dquery, query2, dquery2, keys_w
             return tile
 
         raw = [load_query(0, query)]
+        offsets = sb.tile([P, I // 16], U16, name="offsets")
+        nc.sync.dma_start(offsets[:], offs)
         for r in range(PACK):
             nc.sync.dma_start(key_bytes[r:P:32, :].bitcast(I32), keys_scales[0, r:16:PACK, :].bitcast(I32))
         key_words = sb.tile([P, T], U32, name="key_words", align_bytes=64)
         nc.sync.dma_start(key_words[:].bitcast(I32), keys_words[0].rearrange("p n t -> p (n t)").bitcast(I32))
-        raw.extend([load_query(1, query2), load_query(2, dquery2), load_query(3, dquery)])
+        raw.extend([load_query(1, query2), load_query(2, dquery), load_query(3, dquery2)])
 
         pools = []
         for j in range(E // P):
@@ -90,20 +89,17 @@ def tile_attend_ttproductscore_kernel(tc, query, dquery, query2, dquery2, keys_w
             operand = quantize("q%d" % n, grouped[:].rearrange("p q j -> p (q j)"), Q)
             bank = ps.tile([P, I], F32, name="score%d" % n)
             product(bank[:], operand, listed_keys)
-            if n in (0, 3):
+            if n % 2 == 0:
                 held = sb.tile([P, I], F32, name="score_sb%d" % n, align_bytes=64)
                 nc.scalar.copy(held[:], bank[:])
                 scores.append(held)
             else:
                 scores.append(bank)
-        a, b, tb, ta = scores
+        a, b, ta, tb = scores
 
         factor_rows = ps.tile([P, PACK, P], F32, name="factor_rows")
         for t in range(PACK):
             nc.tensor.transpose(factor_rows[:, t, :], slot_factor[:, t : t + 1].to_broadcast([P, P]), identity[:])
-
-        early = sb.tile([P, PACK * I], BF16, name="early", align_bytes=64)
-        late = sb.tile([P, I], BF16, name="late", align_bytes=64)
 
         def turn(rows, bank_name, grouped):
             pairs = rows.bitcast(F32)
@@ -112,59 +108,76 @@ def tile_attend_ttproductscore_kernel(tc, query, dquery, query2, dquery2, keys_w
                 nc.tensor.transpose(turned[:, u, :], pairs[:, u : I // 2 : 2], identity[:])
             nc.scalar.copy(grouped.bitcast(F32).rearrange("p (e u) -> p e u", u=2), turned[:].rearrange("p u e -> p e u"))
 
-        def gather_values(j, grouped):
-            listed = sb.tile([P, I], BF16, name="v_listed%d" % j, align_bytes=64)
+        def gather_values(j, tag):
+            listed = sb.tile([P, I], BF16, name="v_listed%d" % j, tag=tag, align_bytes=64)
             nc.vector.tensor_copy(listed[:], pools[j][:].indirect(offsets[:]))
-            turn(listed[:], "v_turned%d" % (j % 2), grouped)
-
+            return listed[:]
 
         s = sb.tile([P, I], F32, name="s", align_bytes=64)
         nc.vector.scalar_tensor_tensor(s[:], b[:], 1.0, a[:], ALU.add, ALU.mult)
-        ts_second = sb.tile([P, I], F32, name="ts_second")
-        nc.vector.tensor_tensor(ts_second[:], tb[:], a[:], ALU.mult)
         neg_max = sb.tile([P, 1], F32, name="neg_max")
         nc.vector.tensor_reduce(neg_max[:], s[:], AXIS.X, ALU.max, negate=True)
-        p = sb.tile([P, I], F32, name="p", align_bytes=64)
+        p = sb.tile([P, I], F32, name="p")
         p_sum = sb.tile([P, 1], F32, name="p_sum")
         nc.scalar.activation(p[:], s[:], ACT.Exp, bias=neg_max[:], accum_out=p_sum[:])
+        ts_second = sb.tile([P, I], F32, name="ts_second")
+        nc.vector.tensor_tensor(ts_second[:], tb[:], a[:], ALU.mult)
         ts_first = sb.tile([P, I], F32, name="ts_first")
         nc.vector.scalar_tensor_tensor(ts_first[:], b[:], 1.0, ta[:], ALU.add, ALU.mult)
+        listed_first = gather_values(0, "score_sb0")
 
         pool_bf16 = sb.tile([P, T], BF16, name="pool_bf16", tag="s", align_bytes=64)
         nc.scalar.activation(pool_bf16[:], pools[1][:], ACT.Copy)
-        listed_first = sb.tile([P, I], BF16, name="v_listed1", align_bytes=64)
-        nc.scalar.activation(listed_first[:], pool_bf16[:].indirect(offsets[:]), ACT.Copy)
-        turn(listed_first[:], "v_turned1", early[:, 2 * I : 3 * I])
+        listed_second = sb.tile([P, I], BF16, name="v_listed1", align_bytes=64)
+        nc.scalar.activation(listed_second[:], pool_bf16[:].indirect(offsets[:]), ACT.Copy)
+        early = sb.tile([P, PACK * I], BF16, name="early", tag="vals1", align_bytes=64)
+        turn(listed_first, "v_turned0", early[:, I : 2 * I])
+        turn(listed_second[:], "v_turned1", early[:, 2 * I : 3 * I])
 
-        gather_values(0, early[:, I : 2 * I])
-        ts = sb.tile([P, I], F32, name="ts")
-        nc.vector.tensor_tensor(ts[:], ts_first[:], ts_second[:], ALU.add)
         inv_sum = sb.tile([P, 1], F32, name="inv_sum")
         nc.vector.reciprocal(inv_sum[:], p_sum[:])
+        ts = sb.tile([P, I], F32, name="ts")
+        nc.vector.tensor_tensor(ts[:], ts_first[:], ts_second[:], ALU.add)
+        pno = sb.tile([P, P, PACK], F32, name="pno")
+
+        def scale_weights(words):
+            nc.vector.scalar_tensor_tensor(
+                pno[:, words, :],
+                p[:].rearrange("p (n t) -> p n t", t=PACK)[:, words, :],
+                inv_sum[:],
+                factor_rows[:].rearrange("p t n -> p n t")[:, words, :],
+                ALU.mult,
+                ALU.mult,
+            )
+
+        scale_weights(slice(0, P // 2))
         tpn = sb.tile([P, I], F32, name="tpn")
         mean_ts = sb.tile([P, 1], F32, name="mean_ts")
         nc.vector.scalar_tensor_tensor(tpn[:], ts[:], inv_sum[:], p[:], ALU.mult, ALU.mult, accum_out=mean_ts[:])
-        pno = sb.tile([P, I], F32, name="pno")
-        nc.vector.scalar_tensor_tensor(
-            pno[:].rearrange("p (n t) -> p n t", t=PACK),
-            p[:].rearrange("p (n t) -> p n t", t=PACK),
-            inv_sum[:],
-            factor_rows[:].rearrange("p t n -> p n t"),
-            ALU.mult,
-            ALU.mult,
-        )
+        scale_weights(slice(P // 2, P))
         wo = sb.tile([P, I], BF16, name="wo", align_bytes=64)
-        nc.vector.scalar_tensor_tensor(wo[:], ts[:], mean_ts[:], pno[:], ALU.subtract, ALU.mult)
+        nc.vector.scalar_tensor_tensor(
+            wo[:], ts[:], mean_ts[:], pno[:].rearrange("p n t -> p (n t)"), ALU.subtract, ALU.mult
+        )
         turn(wo[:], "w_turned", early[:, 0:I])
-        gather_values(2, early[:, 3 * I : 4 * I])
-        gather_values(3, late[:])
-        early_codes, early_scales = quantize("early", early[:], I, tag="vals3")
+        turn(gather_values(2, "v_listed2"), "v_turned0", early[:, 3 * I : 4 * I])
+        late = sb.tile([P, I], BF16, name="late", align_bytes=64)
+        turn(gather_values(3, "v_listed3"), "v_turned1", late[:])
+        early_codes = sb.tile([P, I], U32, name="early_codes", tag="vals3", align_bytes=64)
+        early_scales = sb.tile([P, I], U8, name="early_scales", align_bytes=64)
+        for half in range(2):
+            words = slice(half * I // 2, (half + 1) * I // 2)
+            nc.vector.quantize_mx(
+                out=early_codes[:, words].bitcast(FP8X4),
+                scales=early_scales[:, words],
+                in_=early[:, half * 2 * I : (half + 1) * 2 * I],
+            )
         late_codes, late_scales = quantize("late", late[:], P)
 
         weights = (early_codes[:, 0:Q], early_scales[:, 0:Q])
         pieces = (
-            (0, 2 * P, early_codes[:, Q : Q + 2 * P], early_scales[:, Q : Q + 2 * P]),
-            (2 * P, P, early_codes[:, Q + 2 * P : I], early_scales[:, Q + 2 * P : I]),
+            (0, P, early_codes[:, Q : Q + P], early_scales[:, Q : Q + P]),
+            (P, 2 * P, early_codes[:, Q + P : I], early_scales[:, Q + P : I]),
             (3 * P, P, late_codes, late_scales),
         )
         for n, (first, width, codes, scales) in enumerate(pieces):

@@ -30,7 +30,7 @@ def tile_attend_ttproductscore_kernel(tc, query, dquery, query2, dquery2, keys_w
         nc.gpsimd.memset(key_bytes[:].bitcast(I32), 0)
 
         def load_query(n, rows):
-            tile = sb.tile([P, PACK, Q], F32, name="q_raw%d" % n)
+            tile = sb.tile([P, PACK, Q], F32, name="q_raw%d" % n, align_bytes=64)
             nc.sync.dma_start(tile[:], rows.rearrange("(p j) q -> p j q", j=PACK))
             return tile
 
@@ -78,7 +78,7 @@ def tile_attend_ttproductscore_kernel(tc, query, dquery, query2, dquery2, keys_w
         nc.vector.tensor_copy(listed_words[:], key_words[:].indirect(offsets[:]))
         listed_keys = (listed_words[:], listed_bytes[:])
 
-        scores = []
+        queries = []
         for n in range(4):
             grouped = sb.tile([P, Q, PACK], BF16, name="q_grouped%d" % n, align_bytes=64)
             source = raw[n][:].rearrange("p j q -> p q j")
@@ -86,11 +86,14 @@ def tile_attend_ttproductscore_kernel(tc, query, dquery, query2, dquery2, keys_w
                 nc.scalar.activation(grouped[:], source, ACT.Copy)
             else:
                 nc.vector.tensor_copy(grouped[:], source)
-            operand = quantize("q%d" % n, grouped[:].rearrange("p q j -> p (q j)"), Q)
+            queries.append(quantize("q%d" % n, grouped[:].rearrange("p q j -> p (q j)"), Q))
+
+        scores = []
+        for n in range(4):
             bank = ps.tile([P, I], F32, name="score%d" % n)
-            product(bank[:], operand, listed_keys)
+            product(bank[:], queries[n], listed_keys)
             if n % 2 == 0:
-                held = sb.tile([P, I], F32, name="score_sb%d" % n, align_bytes=64)
+                held = sb.tile([P, I], F32, name="score_sb%d" % n, tag="q_raw%d" % (2 - n), align_bytes=64)
                 nc.scalar.copy(held[:], bank[:])
                 scores.append(held)
             else:
@@ -124,7 +127,7 @@ def tile_attend_ttproductscore_kernel(tc, query, dquery, query2, dquery2, keys_w
         nc.vector.tensor_tensor(ts_second[:], tb[:], a[:], ALU.mult)
         ts_first = sb.tile([P, I], F32, name="ts_first")
         nc.vector.scalar_tensor_tensor(ts_first[:], b[:], 1.0, ta[:], ALU.add, ALU.mult)
-        listed_first = gather_values(0, "score_sb0")
+        listed_first = gather_values(0, "q_raw2")
 
         pool_bf16 = sb.tile([P, T], BF16, name="pool_bf16", tag="s", align_bytes=64)
         nc.scalar.activation(pool_bf16[:], pools[1][:], ACT.Copy)
@@ -137,24 +140,19 @@ def tile_attend_ttproductscore_kernel(tc, query, dquery, query2, dquery2, keys_w
         inv_sum = sb.tile([P, 1], F32, name="inv_sum")
         nc.vector.reciprocal(inv_sum[:], p_sum[:])
         ts = sb.tile([P, I], F32, name="ts")
-        nc.vector.tensor_tensor(ts[:], ts_first[:], ts_second[:], ALU.add)
+        nc.gpsimd.tensor_tensor(ts[:], ts_first[:], ts_second[:], ALU.add)
         pno = sb.tile([P, P, PACK], F32, name="pno")
-
-        def scale_weights(words):
-            nc.vector.scalar_tensor_tensor(
-                pno[:, words, :],
-                p[:].rearrange("p (n t) -> p n t", t=PACK)[:, words, :],
-                inv_sum[:],
-                factor_rows[:].rearrange("p t n -> p n t")[:, words, :],
-                ALU.mult,
-                ALU.mult,
-            )
-
-        scale_weights(slice(0, P // 2))
+        nc.vector.scalar_tensor_tensor(
+            pno[:],
+            p[:].rearrange("p (n t) -> p n t", t=PACK),
+            inv_sum[:],
+            factor_rows[:].rearrange("p t n -> p n t"),
+            ALU.mult,
+            ALU.mult,
+        )
         tpn = sb.tile([P, I], F32, name="tpn")
         mean_ts = sb.tile([P, 1], F32, name="mean_ts")
         nc.vector.scalar_tensor_tensor(tpn[:], ts[:], inv_sum[:], p[:], ALU.mult, ALU.mult, accum_out=mean_ts[:])
-        scale_weights(slice(P // 2, P))
         wo = sb.tile([P, I], BF16, name="wo", align_bytes=64)
         nc.vector.scalar_tensor_tensor(
             wo[:], ts[:], mean_ts[:], pno[:].rearrange("p n t -> p (n t)"), ALU.subtract, ALU.mult

from contextlib import ExitStack

import concourse.mybir as mybir
from concourse.masks import make_identity

D, E, T, I, Q = 512, 512, 2048, 512, 128
P = 128
PACK = 4
FLOPS = 2 * (4 * D * Q * I + I * Q * E)

F32 = mybir.dt.float32
BF16 = mybir.dt.bfloat16
I32 = mybir.dt.int32
U32 = mybir.dt.uint32
U16 = mybir.dt.uint16
U8 = mybir.dt.uint8
FP8X4 = mybir.dt.float8_e4m3fn_x4
ALU = mybir.AluOpType
ACT = mybir.ActivationFunctionType
AXIS = mybir.AxisListType


def tile_attend_ttproductscore_kernel(tc, query, dquery, query2, dquery2, keys_words, keys_scales, factors, vals, offs, out):
    nc = tc.nc
    with ExitStack() as ctx:
        sb = ctx.enter_context(tc.tile_pool(name="sb", bufs=1))
        ps = ctx.enter_context(tc.psum_pool(name="ps", bufs=1))

        key_bytes = sb.tile([P, T], U8, name="key_bytes", align_bytes=64)
        nc.gpsimd.memset(key_bytes[:].bitcast(I32), 0)

        def load_query(n, rows):
            tile = sb.tile([P, PACK, Q], F32, name="q_raw%d" % n, align_bytes=64)
            nc.sync.dma_start(tile[:], rows.rearrange("(p j) q -> p j q", j=PACK))
            return tile

        raw = [load_query(0, query)]
        offsets = sb.tile([P, I // 16], U16, name="offsets")
        nc.sync.dma_start(offsets[:], offs)
        for r in range(PACK):
            nc.sync.dma_start(key_bytes[r:P:32, :].bitcast(I32), keys_scales[0, r:16:PACK, :].bitcast(I32))
        key_words = sb.tile([P, T], U32, name="key_words", align_bytes=64)
        nc.sync.dma_start(key_words[:].bitcast(I32), keys_words[0].rearrange("p n t -> p (n t)").bitcast(I32))
        raw.extend([load_query(1, query2), load_query(2, dquery), load_query(3, dquery2)])

        pools = []
        for j in range(E // P):
            tile = sb.tile([P, T], F32, name="vals%d" % j, align_bytes=64)
            nc.sync.dma_start(tile[:], vals[j * P : (j + 1) * P, :])
            pools.append(tile)
            if j == 0:
                slot_factor = sb.tile([P, PACK], F32, name="slot_factor")
                nc.sync.dma_start(slot_factor[:], factors.rearrange("o (p t) -> (o p) t", t=PACK))

        identity = sb.tile([P, P], F32, name="identity")
        make_identity(nc, identity[:])

        def quantize(name, grouped, width, tag=None):
            codes = sb.tile([P, width], U32, name=name + "_codes", tag=tag or name + "_codes", align_bytes=64)
            scales = sb.tile([P, width], U8, name=name + "_scales", align_bytes=64)
            nc.vector.quantize_mx(out=codes[:].bitcast(FP8X4), scales=scales[:], in_=grouped)
            return codes[:], scales[:]

        def product(bank, stationary, moving):
            nc.tensor.matmul_mx(
                out=bank,
                lhsT=stationary[0].bitcast(FP8X4),
                lhsT_scale=stationary[1],
                rhs=moving[0].bitcast(FP8X4),
                rhs_scale=moving[1],
                start=True,
                stop=True,
            )

        listed_bytes = sb.tile([P, I], U8, name="listed_bytes", align_bytes=64)
        nc.vector.tensor_copy(listed_bytes[:], key_bytes[:].indirect(offsets[:]))
        listed_words = sb.tile([P, I], U32, name="listed_words", align_bytes=64)
        nc.vector.tensor_copy(listed_words[:], key_words[:].indirect(offsets[:]))
        listed_keys = (listed_words[:], listed_bytes[:])

        queries = []
        for n in range(4):
            grouped = sb.tile([P, Q, PACK], BF16, name="q_grouped%d" % n, align_bytes=64)
            source = raw[n][:].rearrange("p j q -> p q j")
            if n < 3:
                nc.scalar.activation(grouped[:], source, ACT.Copy)
            else:
                nc.vector.tensor_copy(grouped[:], source)
            queries.append(quantize("q%d" % n, grouped[:].rearrange("p q j -> p (q j)"), Q))

        scores = []
        for n in range(4):
            bank = ps.tile([P, I], F32, name="score%d" % n)
            product(bank[:], queries[n], listed_keys)
            if n % 2 == 0:
                held = sb.tile([P, I], F32, name="score_sb%d" % n, tag="q_raw%d" % (2 - n), align_bytes=64)
                nc.scalar.copy(held[:], bank[:])
                scores.append(held)
            else:
                scores.append(bank)
        a, b, ta, tb = scores

        factor_rows = ps.tile([P, PACK, P], F32, name="factor_rows")
        for t in range(PACK):
            nc.tensor.transpose(factor_rows[:, t, :], slot_factor[:, t : t + 1].to_broadcast([P, P]), identity[:])

        def turn(rows, bank_name, grouped):
            pairs = rows.bitcast(F32)
            turned = ps.tile([P, 2, P], F32, name=bank_name)
            for u in range(2):
                nc.tensor.transpose(turned[:, u, :], pairs[:, u : I // 2 : 2], identity[:])
            nc.scalar.copy(grouped.bitcast(F32).rearrange("p (e u) -> p e u", u=2), turned[:].rearrange("p u e -> p e u"))

        def gather_values(j, tag):
            listed = sb.tile([P, I], BF16, name="v_listed%d" % j, tag=tag, align_bytes=64)
            nc.vector.tensor_copy(listed[:], pools[j][:].indirect(offsets[:]))
            return listed[:]

        s = sb.tile([P, I], F32, name="s", align_bytes=64)
        nc.vector.scalar_tensor_tensor(s[:], b[:], 1.0, a[:], ALU.add, ALU.mult)
        neg_max = sb.tile([P, 1], F32, name="neg_max")
        nc.vector.tensor_reduce(neg_max[:], s[:], AXIS.X, ALU.max, negate=True)
        p = sb.tile([P, I], F32, name="p")
        p_sum = sb.tile([P, 1], F32, name="p_sum")
        nc.scalar.activation(p[:], s[:], ACT.Exp, bias=neg_max[:], accum_out=p_sum[:])
        ts_second = sb.tile([P, I], F32, name="ts_second")
        nc.vector.tensor_tensor(ts_second[:], tb[:], a[:], ALU.mult)
        ts_first = sb.tile([P, I], F32, name="ts_first")
        nc.vector.scalar_tensor_tensor(ts_first[:], b[:], 1.0, ta[:], ALU.add, ALU.mult)
        listed_first = gather_values(0, "q_raw2")

        pool_bf16 = sb.tile([P, T], BF16, name="pool_bf16", tag="s", align_bytes=64)
        nc.scalar.activation(pool_bf16[:], pools[1][:], ACT.Copy)
        listed_second = sb.tile([P, I], BF16, name="v_listed1", align_bytes=64)
        nc.scalar.activation(listed_second[:], pool_bf16[:].indirect(offsets[:]), ACT.Copy)
        early = sb.tile([P, PACK * I], BF16, name="early", tag="vals1", align_bytes=64)
        turn(listed_first, "v_turned0", early[:, I : 2 * I])
        turn(listed_second[:], "v_turned1", early[:, 2 * I : 3 * I])

        inv_sum = sb.tile([P, 1], F32, name="inv_sum")
        nc.vector.reciprocal(inv_sum[:], p_sum[:])
        ts = sb.tile([P, I], F32, name="ts")
        nc.gpsimd.tensor_tensor(ts[:], ts_first[:], ts_second[:], ALU.add)
        pno = sb.tile([P, P, PACK], F32, name="pno")
        nc.vector.scalar_tensor_tensor(
            pno[:],
            p[:].rearrange("p (n t) -> p n t", t=PACK),
            inv_sum[:],
            factor_rows[:].rearrange("p t n -> p n t"),
            ALU.mult,
            ALU.mult,
        )
        tpn = sb.tile([P, I], F32, name="tpn")
        mean_ts = sb.tile([P, 1], F32, name="mean_ts")
        nc.vector.scalar_tensor_tensor(tpn[:], ts[:], inv_sum[:], p[:], ALU.mult, ALU.mult, accum_out=mean_ts[:])
        wo = sb.tile([P, I], BF16, name="wo", align_bytes=64)
        nc.vector.scalar_tensor_tensor(
            wo[:], ts[:], mean_ts[:], pno[:].rearrange("p n t -> p (n t)"), ALU.subtract, ALU.mult
        )
        turn(wo[:], "w_turned", early[:, 0:I])
        turn(gather_values(2, "v_listed2"), "v_turned0", early[:, 3 * I : 4 * I])
        late = sb.tile([P, I], BF16, name="late", align_bytes=64)
        turn(gather_values(3, "v_listed3"), "v_turned1", late[:])
        early_codes = sb.tile([P, I], U32, name="early_codes", tag="vals3", align_bytes=64)
        early_scales = sb.tile([P, I], U8, name="early_scales", align_bytes=64)
        for half in range(2):
            words = slice(half * I // 2, (half + 1) * I // 2)
            nc.vector.quantize_mx(
                out=early_codes[:, words].bitcast(FP8X4),
                scales=early_scales[:, words],
                in_=early[:, half * 2 * I : (half + 1) * 2 * I],
            )
        late_codes, late_scales = quantize("late", late[:], P)

        weights = (early_codes[:, 0:Q], early_scales[:, 0:Q])
        pieces = (
            (0, P, early_codes[:, Q : Q + P], early_scales[:, Q : Q + P]),
            (P, 2 * P, early_codes[:, Q + P : I], early_scales[:, Q + P : I]),
            (3 * P, P, late_codes, late_scales),
        )
        for n, (first, width, codes, scales) in enumerate(pieces):
            bank = ps.tile([P, width], F32, name="score%d" % n)
            product(bank[:], weights, (codes, scales))
            result = sb.tile([P, width], F32, name="result%d" % n)
            nc.scalar.copy(result[:], bank[:])
            nc.sync.dma_start(out[:, first : first + width], result[:])
